import numpy as np, ml_dtypes
CORES = [5,21,45,77,85,101,109,125,133,141,189,213]
N = 12
DEG, TK, TIMES = 3, 512, 3
MASK = [[11,0,1],[0,1,2],[1,2,3],[2,3,4],[3,4,5],[4,5,6],[5,6,7],[6,7,8],[7,8,9],[8,9,10],[9,10,11],[10,11,0]]
def setup_inputs(rng):
    return {"x": rng.standard_normal((N, 128, TK), dtype=np.float32).astype(ml_dtypes.bfloat16), "w": (rng.standard_normal((N, 128, DEG * 128), dtype=np.float32) / np.float32(np.sqrt(128 * DEG / 2))).astype(ml_dtypes.bfloat16)}
def setup_inputs_big(rng):
    d = setup_inputs(rng)
    for k in ("x",): d[k] = (d[k].astype(np.float32) * 1048576.0).astype(d[k].dtype)
    return d
def setup_inputs_small(rng):
    d = setup_inputs(rng)
    for k in ("x",): d[k] = (d[k].astype(np.float32) * (1 / 1048576.0)).astype(d[k].dtype)
    return d
def setup_inputs_apart(rng):
    d = setup_inputs(rng)
    f = (10.0 ** rng.permutation(np.linspace(-1.5, 1.5, N))).astype(np.float32).reshape(N, 1, 1)
    for k in ("x",): d[k] = (d[k].astype(np.float32) * f).astype(d[k].dtype)
    return d
def reference(x, w):
    X, W = x.astype(np.float64), w.astype(np.float64)
    h = list(X)
    for _ in range(TIMES):
        h = [sum(W[r][:, 128 * i:128 * i + 128].T @ h[j] for i, j in enumerate(MASK[r])) for r in range(N)]
    return {"y": np.stack(h).astype(ml_dtypes.bfloat16)}

@@ -1,0 +1,168 @@
+from concourse.bass import DstId, RemoteDMATransfer
+
+COLS, TILE, DEG = 512, 128, 3
+Q = 4
+NCOL = COLS // Q
+
+SCRATCH = {
+    "xs": ("sbuf", [128, COLS], "bfloat16"),
+    "ws": ("sbuf", [128, DEG * TILE], "bfloat16"),
+    "ys": ("sbuf", [128, COLS], "bfloat16"),
+}
+for _t in range(3):
+    SCRATCH["o%d" % _t] = ("sbuf", [128, NCOL], "bfloat16")
+for _i in range(DEG):
+    SCRATCH["l0_%d" % _i] = ("sbuf", [128, NCOL], "bfloat16")
+    SCRATCH["l1_%d" % _i] = ("sbuf", [128, NCOL], "bfloat16")
+    SCRATCH["f%d" % _i] = ("sbuf", [128, COLS], "bfloat16")
+for _q in range(max(Q, 2)):
+    SCRATCH["p%d" % _q] = ("psum", [128, 512], "float32")
+
+SEMAPHORES = (["ldx", "ldw", "ox", "wl", "sent", "st", "mm0", "mm1", "cp1", "cp2"]
+              + ["a%d_%d" % (t, i) for t in range(2) for i in range(DEG)]
+              + ["g%d_%d" % (q, i) for q in range(Q) for i in range(DEG)]
+              + ["mf%d" % q for q in range(Q)] + ["cf%d" % q for q in range(Q)])
+
+
+def _count(mask):
+    return bin(mask).count("1")
+
+
+def _workers(topo, home):
+    span = 2 * topo.CORES_PER_CHIP
+    near = range(max(0, home - span), home + span)
+    here = [c for c in near if c != home and (topo.host(c), topo.chip(c)) == (topo.host(home), topo.chip(home))]
+    across = [c for c in near if topo.mates(home, c)][0]
+    own = sorted([c for c in here if topo.may_write(c, across)], key=lambda c: (topo.die(c), c))
+    return own[::len(own) // Q][:Q]
+
+
+def _fan(topo, src, dsts, avoid=0):
+    common = ~avoid
+    for d in dsts:
+        common &= topo.mask(src, d)
+    lanes = [b for b in range(common.bit_length()) if (common >> b) & 1]
+    per = 1
+    while per * 2 * len(dsts) <= len(lanes):
+        per *= 2
+    return [sum(1 << b for b in lanes[k * per:(k + 1) * per]) for k in range(len(dsts))]
+
+
+def _post(g, topo, core, items, local_sem, avoid=0):
+    masks = _fan(topo, core, [it[0] for it in items], avoid)
+    trs = []
+    for (dst, src_ap, dst_ap, sem), m in zip(items, masks):
+        rid, pid = topo.addr(dst, core)
+        trs.append(RemoteDMATransfer(dst_ids=[DstId(rid=rid, pnc=pid)], dma_engine_mask=m, remote_sem=sem,
+                                     src=src_ap, dst=dst_ap))
+    g.remote_dma_fused(trs, local_sem=local_sem)
+    used = 0
+    for m in masks:
+        used |= m
+    return sum(_count(m) for m in masks), used
+
+
+def _far(topo, a, b):
+    if a == b:
+        return 0
+    if topo.mates(a, b):
+        return 1
+    return 2 if topo.same_plane(a, b) else 3
+
+
+def rank_program(g, core, T, topo):
+    tab = T.tables["MASK"]
+    homes = list(T.cores)
+    n = len(homes)
+    workers = [_workers(topo, h) for h in homes]
+    takers = [[(d, i) for d in range(n) for i in range(DEG) if tab[d][i] == r and d != r] for r in range(n)]
+    S = T.sem
+
+    def tile(i):
+        return T.ws[:, i * TILE:(i + 1) * TILE]
+
+    def order(r):
+        return sorted(range(DEG), key=lambda i: _far(topo, homes[r], homes[tab[r][i]]))
+
+    def lanes_w(j, q):
+        return _count(_fan(topo, workers[j][q], [workers[d][q] for d, _ in takers[j]])[0])
+
+    def lanes_h(j, q):
+        return _count(_fan(topo, workers[j][q], [homes[d] for d, _ in takers[j]])[0])
+
+    def lanes_own(j, q):
+        busy = 0
+        for m in _fan(topo, workers[j][q], [homes[d] for d, _ in takers[j]]):
+            busy |= m
+        return _count(_fan(topo, workers[j][q], [homes[j]], busy)[0])
+
+    r = T.rank_of(core)
+    if r is not None:
+        g.sync.dma_start(T.xs[:], T.x[:]).then_inc(S.ldx, 16)
+        g.scalar.dma_start(T.ws[:], T.w[:]).then_inc(S.ldw, 16)
+        sent = 0
+        g.wait_ge(S.ldx, 16)
+        k, _ = _post(g, topo, core, [(workers[r][q], T.xs[:, q * NCOL:(q + 1) * NCOL], T.o0[:], S.ox)
+                                     for q in range(Q)], S.sent)
+        sent += k
+        g.wait_ge(S.ldw, 16)
+        k, _ = _post(g, topo, core, [(workers[r][q], T.ws[:], T.ws[:], S.wl) for q in range(Q)], S.sent)
+        sent += k
+        g.tensor.wait_ge(S.ldw, 16)
+        terms = order(r)
+        for k, i in enumerate(terms):
+            j = tab[r][i]
+            for q in range(Q):
+                g.tensor.wait_ge(S["g%d_%d" % (q, i)], lanes_own(j, q) if j == r else lanes_h(j, q))
+                g.tensor.matmul(T["p%d" % q][:, 0:NCOL], tile(i), T["f%d" % i][:, q * NCOL:(q + 1) * NCOL],
+                                start=(k == 0), stop=(k == DEG - 1)).then_inc(S["mf%d" % q], 1)
+        for q in range(Q):
+            g.vector.wait_ge(S["mf%d" % q], DEG)
+            g.vector.tensor_copy(T.ys[:, q * NCOL:(q + 1) * NCOL], T["p%d" % q][:, 0:NCOL]).then_inc(S["cf%d" % q], 1)
+        for q in range(Q):
+            g.sync.wait_ge(S["cf%d" % q], 1)
+        g.sync.dma_start(T.y[:], T.ys[:]).then_inc(S.st, 16)
+        g.sync.wait_ge(S.st, 16)
+        g.wait_ge(S.sent, sent)
+        return
+
+    for r in range(n):
+        if core not in workers[r]:
+            continue
+        q = workers[r].index(core)
+        from_home = _count(_fan(topo, homes[r], workers[r])[q])
+        terms = order(r)
+        sent = 0
+        for t in range(2):
+            own = T["o%d" % t]
+            ready, val = (S.ox, from_home) if t == 0 else (S.cp1, 1)
+            g.wait_ge(ready, val)
+            k, _ = _post(g, topo, core, [(workers[d][q], own[:], T["l%d_%d" % (t, i)][:], S["a%d_%d" % (t, i)])
+                                         for d, i in takers[r]], S.sent)
+            sent += k
+            if t == 0:
+                g.tensor.wait_ge(S.wl, from_home)
+            for k, i in enumerate(terms):
+                j = tab[r][i]
+                if j == r:
+                    g.tensor.wait_ge(ready, val)
+                    rhs = own[:]
+                else:
+                    g.tensor.wait_ge(S["a%d_%d" % (t, i)], lanes_w(j, q))
+                    rhs = T["l%d_%d" % (t, i)][:]
+                g.tensor.matmul(T["p%d" % t][:, 0:NCOL], tile(i), rhs,
+                                start=(k == 0), stop=(k == DEG - 1)).then_inc(S["mm%d" % t], 1)
+            g.vector.wait_ge(S["mm%d" % t], DEG)
+            g.vector.tensor_copy(T["o%d" % (t + 1)][:], T["p%d" % t][:, 0:NCOL]).then_inc(S["cp%d" % (t + 1)], 1)
+        g.wait_ge(S.cp2, 1)
+        cols = slice(q * NCOL, (q + 1) * NCOL)
+        k, busy = _post(g, topo, core, [(homes[d], T.o2[:], T["f%d" % i][:, cols], S["g%d_%d" % (q, i)])
+                                        for d, i in takers[r]], S.sent)
+        sent += k
+        mine = [i for i in range(DEG) if tab[r][i] == r]
+        for i in mine:
+            k, _ = _post(g, topo, core, [(homes[r], T.o2[:], T["f%d" % i][:, cols], S["g%d_%d" % (q, i)])],
+                         S.sent, busy)
+            sent += k
+        g.wait_ge(S.sent, sent)
+        return

@@ -1,27 +1,37 @@
 from concourse.bass import DstId, RemoteDMATransfer
+from concourse.mybir import AluOpType
 
 COLS, TILE, DEG = 512, 128, 3
 Q = 4
 NCOL = COLS // Q
+SUP = 2 * DEG - 1
+HALF = DEG * TILE // 2
 
 SCRATCH = {
     "xs": ("sbuf", [128, COLS], "bfloat16"),
     "ws": ("sbuf", [128, DEG * TILE], "bfloat16"),
     "ys": ("sbuf", [128, COLS], "bfloat16"),
+    "ones": ("sbuf", [128, TILE], "bfloat16"),
+    "idn": ("sbuf", [128, TILE], "bfloat16"),
+    "bt": ("sbuf", [128, SUP * TILE], "bfloat16"),
+    "o0": ("sbuf", [128, NCOL], "bfloat16"),
+    "o1": ("sbuf", [128, NCOL], "bfloat16"),
 }
-for _t in range(3):
-    SCRATCH["o%d" % _t] = ("sbuf", [128, NCOL], "bfloat16")
 for _i in range(DEG):
     SCRATCH["l0_%d" % _i] = ("sbuf", [128, NCOL], "bfloat16")
-    SCRATCH["l1_%d" % _i] = ("sbuf", [128, NCOL], "bfloat16")
-    SCRATCH["f%d" % _i] = ("sbuf", [128, COLS], "bfloat16")
-for _q in range(max(Q, 2)):
-    SCRATCH["p%d" % _q] = ("psum", [128, 512], "float32")
+    SCRATCH["wn%d" % _i] = ("sbuf", [128, DEG * TILE], "bfloat16")
+    SCRATCH["wt%d" % _i] = ("sbuf", [128, DEG * TILE], "bfloat16")
+    SCRATCH["t%d" % _i] = ("psum", [128, 1024], "bfloat16")
+for _s in range(SUP):
+    SCRATCH["f%d" % _s] = ("sbuf", [128, COLS], "bfloat16")
+    SCRATCH["p%d" % _s] = ("psum", [128, 512], "float32")
 
-SEMAPHORES = (["ldx", "ldw", "ox", "wl", "sent", "st", "mm0", "mm1", "cp1", "cp2"]
-              + ["a%d_%d" % (t, i) for t in range(2) for i in range(DEG)]
-              + ["g%d_%d" % (q, i) for q in range(Q) for i in range(DEG)]
-              + ["mf%d" % q for q in range(Q)] + ["cf%d" % q for q in range(Q)])
+SEMAPHORES = (["ldx0", "ldx1", "ldw", "ox", "wl", "sent", "mm0", "cp1", "one", "idn", "bc"]
+              + ["a0_%d" % i for i in range(DEG)] + ["wa%d" % i for i in range(DEG)]
+              + ["tr%d" % i for i in range(DEG)] + ["tc%d" % i for i in range(DEG)]
+              + ["bm%d" % s for s in range(SUP)]
+              + ["g%d_%d" % (q, s) for q in range(Q) for s in range(SUP)]
+              + ["mf%d" % q for q in range(Q)] + ["cf%d" % q for q in range(Q)] + ["st%d" % q for q in range(Q)])
 
 
 def _count(mask):
@@ -37,7 +47,7 @@ def _workers(topo, home):
     return own[::len(own) // Q][:Q]
 
 
-def _fan(topo, src, dsts, avoid=0):
+def _fan(topo, src, dsts, avoid=0, turn=False):
     common = ~avoid
     for d in dsts:
         common &= topo.mask(src, d)
@@ -45,11 +55,13 @@ def _fan(topo, src, dsts, avoid=0):
     per = 1
     while per * 2 * len(dsts) <= len(lanes):
         per *= 2
+    if turn:
+        return [sum(1 << b for b in lanes[k::len(dsts)][:per]) for k in range(len(dsts))]
     return [sum(1 << b for b in lanes[k * per:(k + 1) * per]) for k in range(len(dsts))]
 
 
-def _post(g, topo, core, items, local_sem, avoid=0):
-    masks = _fan(topo, core, [it[0] for it in items], avoid)
+def _post(g, topo, core, items, local_sem, avoid=0, turn=False):
+    masks = _fan(topo, core, [it[0] for it in items], avoid, turn)
     trs = []
     for (dst, src_ap, dst_ap, sem), m in zip(items, masks):
         rid, pid = topo.addr(dst, core)
@@ -75,8 +87,24 @@ def rank_program(g, core, T, topo):
     homes = list(T.cores)
     n = len(homes)
     workers = [_workers(topo, h) for h in homes]
-    takers = [[(d, i) for d in range(n) for i in range(DEG) if tab[d][i] == r and d != r] for r in range(n)]
     S = T.sem
+    takers = [[(d, i) for d in range(n) for i in range(DEG) if tab[d][i] == r and d != r] for r in range(n)]
+    sup = []
+    for d in range(n):
+        lst = []
+        for i in range(DEG):
+            for k in range(DEG):
+                if tab[tab[d][i]][k] not in lst:
+                    lst.append(tab[tab[d][i]][k])
+        sup.append(lst)
+    takers2 = [[(d, sup[d].index(r)) for d in range(n) if d != r and r in sup[d]] for r in range(n)]
+    direct = [[(d, i) for d, i in takers[r] if topo.may_write(homes[r], homes[d])] for r in range(n)]
+    cross = [sorted([(d, i) for d, i in takers[r] if not topo.may_write(homes[r], homes[d])],
+                    key=lambda e: -_far(topo, homes[r], homes[e[0]])) for r in range(n)]
+
+    def col(q):
+        c = (q % 2) * (Q // 2) + q // 2
+        return slice(c * NCOL, (c + 1) * NCOL)
 
     def tile(i):
         return T.ws[:, i * TILE:(i + 1) * TILE]
@@ -88,41 +116,98 @@ def rank_program(g, core, T, topo):
         return _count(_fan(topo, workers[j][q], [workers[d][q] for d, _ in takers[j]])[0])
 
     def lanes_h(j, q):
-        return _count(_fan(topo, workers[j][q], [homes[d] for d, _ in takers[j]])[0])
+        return _count(_fan(topo, workers[j][q], [homes[d] for d, _ in takers2[j]])[0])
 
     def lanes_own(j, q):
         busy = 0
-        for m in _fan(topo, workers[j][q], [homes[d] for d, _ in takers[j]]):
+        for m in _fan(topo, workers[j][q], [homes[d] for d, _ in takers2[j]]):
             busy |= m
         return _count(_fan(topo, workers[j][q], [homes[j]], busy)[0])
 
+    def w_lands(j, d):
+        if topo.may_write(homes[j], homes[d]):
+            return _count(_fan(topo, homes[j], [homes[e] for e, _ in direct[j]])[0])
+        for a in range(2):
+            part = cross[j][a::2]
+            if d in [e for e, _ in part]:
+                return sum(_count(_fan(topo, workers[j][q], [homes[e] for e, _ in part])[0]) for q in range(a, Q, 2))
+
     r = T.rank_of(core)
     if r is not None:
-        g.sync.dma_start(T.xs[:], T.x[:]).then_inc(S.ldx, 16)
-        g.scalar.dma_start(T.ws[:], T.w[:]).then_inc(S.ldw, 16)
+        for a in range(2):
+            wave = slice(a * COLS // 2, (a + 1) * COLS // 2)
+            g.sync.dma_start(T.xs[:, wave], T.x[:, wave]).then_inc(S["ldx%d" % a], 16)
+        g.sync.dma_start(T.ws[:], T.w[:]).then_inc(S.ldw, 16)
+        g.vector.memset(T.ones[:], 1.0).then_inc(S.one, 1)
+        g.wait_ge(S.one, 1)
+        g.affine_select(T.idn[:], T.ones[:], [[-1, TILE]], AluOpType.is_equal, 0.0, 0, 1).then_inc(S.idn, 1)
         sent = 0
-        g.wait_ge(S.ldx, 16)
-        k, _ = _post(g, topo, core, [(workers[r][q], T.xs[:, q * NCOL:(q + 1) * NCOL], T.o0[:], S.ox)
-                                     for q in range(Q)], S.sent)
-        sent += k
+        for a in range(2):
+            g.wait_ge(S["ldx%d" % a], 16)
+            k, _ = _post(g, topo, core, [(workers[r][q], T.xs[:, col(q)], T.o0[:], S.ox) for q in range(a, Q, 2)],
+                         S.sent, turn=True)
+            sent += k
         g.wait_ge(S.ldw, 16)
-        k, _ = _post(g, topo, core, [(workers[r][q], T.ws[:], T.ws[:], S.wl) for q in range(Q)], S.sent)
-        sent += k
+        for a in range(2):
+            k, _ = _post(g, topo, core, [(workers[r][q], T.ws[:], T.ws[:], S.wl) for q in range(a, Q, 2)], S.sent,
+                         turn=True)
+            sent += k
+        if direct[r]:
+            k, _ = _post(g, topo, core, [(homes[d], T.ws[:], T["wn%d" % i][:], S["wa%d" % i]) for d, i in direct[r]],
+                         S.sent)
+            sent += k
+        mine = sup[r]
+        total = [0] * len(mine)
+        for i in range(DEG):
+            for k in range(DEG):
+                total[mine.index(tab[tab[r][i]][k])] += 1
+        seen = [0] * len(mine)
+        copied = [False] * len(mine)
         g.tensor.wait_ge(S.ldw, 16)
-        terms = order(r)
-        for k, i in enumerate(terms):
+        g.tensor.wait_ge(S.idn, 1)
+        for i in order(r):
             j = tab[r][i]
-            for q in range(Q):
-                g.tensor.wait_ge(S["g%d_%d" % (q, i)], lanes_own(j, q) if j == r else lanes_h(j, q))
-                g.tensor.matmul(T["p%d" % q][:, 0:NCOL], tile(i), T["f%d" % i][:, q * NCOL:(q + 1) * NCOL],
-                                start=(k == 0), stop=(k == DEG - 1)).then_inc(S["mf%d" % q], 1)
-        for q in range(Q):
-            g.vector.wait_ge(S["mf%d" % q], DEG)
-            g.vector.tensor_copy(T.ys[:, q * NCOL:(q + 1) * NCOL], T["p%d" % q][:, 0:NCOL]).then_inc(S["cf%d" % q], 1)
-        for q in range(Q):
-            g.sync.wait_ge(S["cf%d" % q], 1)
-        g.sync.dma_start(T.y[:], T.ys[:]).then_inc(S.st, 16)
-        g.sync.wait_ge(S.st, 16)
+            if j == r:
+                wb = T.ws
+            else:
+                g.tensor.wait_ge(S["wa%d" % i], w_lands(j, r))
+                wb = T["wn%d" % i]
+            for k in range(DEG):
+                g.tensor.transpose(T["t%d" % i][:, k * TILE:(k + 1) * TILE], wb[:, k * TILE:(k + 1) * TILE],
+                                   T.idn[:]).then_inc(S["tr%d" % i], 1)
+            g.vector.wait_ge(S["tr%d" % i], DEG)
+            g.vector.tensor_copy(T["wt%d" % i][:], T["t%d" % i][:, 0:DEG * TILE]).then_inc(S["tc%d" % i], 1)
+            g.tensor.wait_ge(S["tc%d" % i], 1)
+            for k in range(DEG):
+                s = mine.index(tab[j][k])
+                g.tensor.matmul(T["p%d" % s][:, 0:TILE], T["wt%d" % i][:, k * TILE:(k + 1) * TILE], tile(i),
+                                start=(seen[s] == 0), stop=(seen[s] == total[s] - 1)).then_inc(S["bm%d" % s], 1)
+                seen[s] += 1
+            for s in range(len(mine)):
+                if seen[s] == total[s] and not copied[s]:
+                    copied[s] = True
+                    g.vector.wait_ge(S["bm%d" % s], total[s])
+                    g.vector.tensor_copy(T.bt[:, s * TILE:(s + 1) * TILE], T["p%d" % s][:, 0:TILE]).then_inc(S.bc, 1)
+        g.tensor.wait_ge(S.bc, len(mine))
+        terms = sorted(range(len(mine)), key=lambda s: _far(topo, homes[r], homes[mine[s]]))
+        inturn = [q for a in range(2) for q in range(a, Q, 2)]
+        for a in range(2):
+            for k, s in enumerate(terms):
+                m = mine[s]
+                for q in range(a, Q, 2):
+                    g.tensor.wait_ge(S["g%d_%d" % (q, s)], lanes_own(m, q) if m == r else lanes_h(m, q))
+                    g.tensor.matmul(T["p%d" % q][:, 0:NCOL], T.bt[:, s * TILE:(s + 1) * TILE], T["f%d" % s][:, col(q)],
+                                    start=(k == 0), stop=(k == len(terms) - 1)).then_inc(S["mf%d" % q], 1)
+        for q in inturn:
+            g.vector.wait_ge(S["mf%d" % q], len(terms))
+            g.vector.tensor_copy(T.ys[:, col(q)], T["p%d" % q][:, 0:NCOL]).then_inc(S["cf%d" % q], 1)
+        for q in inturn:
+            eng = g.sync if q // 2 == 0 else g.scalar
+            eng.wait_ge(S["cf%d" % q], 1)
+            eng.dma_start(T.y[:, col(q)], T.ys[:, col(q)]).then_inc(S["st%d" % q], 16)
+        for q in inturn:
+            eng = g.sync if q // 2 == 0 else g.scalar
+            eng.wait_ge(S["st%d" % q], 16)
         g.wait_ge(S.sent, sent)
         return
 
@@ -130,38 +215,41 @@ def rank_program(g, core, T, topo):
         if core not in workers[r]:
             continue
         q = workers[r].index(core)
-        from_home = _count(_fan(topo, homes[r], workers[r])[q])
-        terms = order(r)
+        x_lands = _count(_fan(topo, homes[r], workers[r][q % 2::2])[0])
+        wl_lands = x_lands
         sent = 0
-        for t in range(2):
-            own = T["o%d" % t]
-            ready, val = (S.ox, from_home) if t == 0 else (S.cp1, 1)
-            g.wait_ge(ready, val)
-            k, _ = _post(g, topo, core, [(workers[d][q], own[:], T["l%d_%d" % (t, i)][:], S["a%d_%d" % (t, i)])
-                                         for d, i in takers[r]], S.sent)
-            sent += k
-            if t == 0:
-                g.tensor.wait_ge(S.wl, from_home)
-            for k, i in enumerate(terms):
-                j = tab[r][i]
-                if j == r:
-                    g.tensor.wait_ge(ready, val)
-                    rhs = own[:]
-                else:
-                    g.tensor.wait_ge(S["a%d_%d" % (t, i)], lanes_w(j, q))
-                    rhs = T["l%d_%d" % (t, i)][:]
-                g.tensor.matmul(T["p%d" % t][:, 0:NCOL], tile(i), rhs,
-                                start=(k == 0), stop=(k == DEG - 1)).then_inc(S["mm%d" % t], 1)
-            g.vector.wait_ge(S["mm%d" % t], DEG)
-            g.vector.tensor_copy(T["o%d" % (t + 1)][:], T["p%d" % t][:, 0:NCOL]).then_inc(S["cp%d" % (t + 1)], 1)
-        g.wait_ge(S.cp2, 1)
-        cols = slice(q * NCOL, (q + 1) * NCOL)
-        k, busy = _post(g, topo, core, [(homes[d], T.o2[:], T["f%d" % i][:, cols], S["g%d_%d" % (q, i)])
-                                        for d, i in takers[r]], S.sent)
+        g.wait_ge(S.ox, x_lands)
+        k, _ = _post(g, topo, core, [(workers[d][q], T.o0[:], T["l0_%d" % i][:], S["a0_%d" % i])
+                                     for d, i in takers[r]], S.sent)
         sent += k
-        mine = [i for i in range(DEG) if tab[r][i] == r]
-        for i in mine:
-            k, _ = _post(g, topo, core, [(homes[r], T.o2[:], T["f%d" % i][:, cols], S["g%d_%d" % (q, i)])],
+        part = cross[r][q % 2::2]
+        if part:
+            half = slice((q // 2) * HALF, (q // 2 + 1) * HALF)
+            g.wait_ge(S.wl, wl_lands)
+            k, _ = _post(g, topo, core, [(homes[d], T.ws[:, half], T["wn%d" % i][:, half], S["wa%d" % i])
+                                         for d, i in part], S.sent)
+            sent += k
+        g.tensor.wait_ge(S.wl, wl_lands)
+        terms = order(r)
+        for k, i in enumerate(terms):
+            j = tab[r][i]
+            if j == r:
+                g.tensor.wait_ge(S.ox, x_lands)
+                rhs = T.o0[:]
+            else:
+                g.tensor.wait_ge(S["a0_%d" % i], lanes_w(j, q))
+                rhs = T["l0_%d" % i][:]
+            g.tensor.matmul(T.p0[:, 0:NCOL], tile(i), rhs, start=(k == 0), stop=(k == DEG - 1)).then_inc(S.mm0, 1)
+        g.vector.wait_ge(S.mm0, DEG)
+        g.vector.tensor_copy(T.o1[:], T.p0[:, 0:NCOL]).then_inc(S.cp1, 1)
+        g.wait_ge(S.cp1, 1)
+        cols = col(q)
+        k, busy = _post(g, topo, core, [(homes[d], T.o1[:], T["f%d" % s][:, cols], S["g%d_%d" % (q, s)])
+                                        for d, s in takers2[r]], S.sent)
+        sent += k
+        if r in sup[r]:
+            s = sup[r].index(r)
+            k, _ = _post(g, topo, core, [(homes[r], T.o1[:], T["f%d" % s][:, cols], S["g%d_%d" % (q, s)])],
                          S.sent, busy)
             sent += k
         g.wait_ge(S.sent, sent)

from concourse.bass import DstId, RemoteDMATransfer
from concourse.mybir import AluOpType

COLS, TILE, DEG = 512, 128, 3
Q = 4
NCOL = COLS // Q
SUP = 2 * DEG - 1
HALF = DEG * TILE // 2

SCRATCH = {
    "xs": ("sbuf", [128, COLS], "bfloat16"),
    "ws": ("sbuf", [128, DEG * TILE], "bfloat16"),
    "ys": ("sbuf", [128, COLS], "bfloat16"),
    "ones": ("sbuf", [128, TILE], "bfloat16"),
    "idn": ("sbuf", [128, TILE], "bfloat16"),
    "bt": ("sbuf", [128, SUP * TILE], "bfloat16"),
    "o0": ("sbuf", [128, NCOL], "bfloat16"),
    "o1": ("sbuf", [128, NCOL], "bfloat16"),
}
for _i in range(DEG):
    SCRATCH["l0_%d" % _i] = ("sbuf", [128, NCOL], "bfloat16")
    SCRATCH["wn%d" % _i] = ("sbuf", [128, DEG * TILE], "bfloat16")
    SCRATCH["wt%d" % _i] = ("sbuf", [128, DEG * TILE], "bfloat16")
    SCRATCH["t%d" % _i] = ("psum", [128, 1024], "bfloat16")
for _s in range(SUP):
    SCRATCH["f%d" % _s] = ("sbuf", [128, COLS], "bfloat16")
    SCRATCH["p%d" % _s] = ("psum", [128, 512], "float32")

SEMAPHORES = (["ldx0", "ldx1", "ldw", "ox", "wl", "sent", "mm0", "cp1", "one", "idn", "bc"]
              + ["a0_%d" % i for i in range(DEG)] + ["wa%d" % i for i in range(DEG)]
              + ["tr%d" % i for i in range(DEG)] + ["tc%d" % i for i in range(DEG)]
              + ["bm%d" % s for s in range(SUP)]
              + ["g%d_%d" % (q, s) for q in range(Q) for s in range(SUP)]
              + ["mf%d" % q for q in range(Q)] + ["cf%d" % q for q in range(Q)] + ["st%d" % q for q in range(Q)])


def _count(mask):
    return bin(mask).count("1")


def _workers(topo, home):
    span = 2 * topo.CORES_PER_CHIP
    near = range(max(0, home - span), home + span)
    here = [c for c in near if c != home and (topo.host(c), topo.chip(c)) == (topo.host(home), topo.chip(home))]
    across = [c for c in near if topo.mates(home, c)][0]
    own = sorted([c for c in here if topo.may_write(c, across)], key=lambda c: (topo.die(c), c))
    return own[::len(own) // Q][:Q]


def _fan(topo, src, dsts, avoid=0, turn=False):
    common = ~avoid
    for d in dsts:
        common &= topo.mask(src, d)
    lanes = [b for b in range(common.bit_length()) if (common >> b) & 1]
    per = 1
    while per * 2 * len(dsts) <= len(lanes):
        per *= 2
    if turn:
        return [sum(1 << b for b in lanes[k::len(dsts)][:per]) for k in range(len(dsts))]
    return [sum(1 << b for b in lanes[k * per:(k + 1) * per]) for k in range(len(dsts))]


def _post(g, topo, core, items, local_sem, avoid=0, turn=False):
    masks = _fan(topo, core, [it[0] for it in items], avoid, turn)
    trs = []
    for (dst, src_ap, dst_ap, sem), m in zip(items, masks):
        rid, pid = topo.addr(dst, core)
        trs.append(RemoteDMATransfer(dst_ids=[DstId(rid=rid, pnc=pid)], dma_engine_mask=m, remote_sem=sem,
                                     src=src_ap, dst=dst_ap))
    g.remote_dma_fused(trs, local_sem=local_sem)
    used = 0
    for m in masks:
        used |= m
    return sum(_count(m) for m in masks), used


def _far(topo, a, b):
    if a == b:
        return 0
    if topo.mates(a, b):
        return 1
    return 2 if topo.same_plane(a, b) else 3


def rank_program(g, core, T, topo):
    tab = T.tables["MASK"]
    homes = list(T.cores)
    n = len(homes)
    workers = [_workers(topo, h) for h in homes]
    S = T.sem
    takers = [[(d, i) for d in range(n) for i in range(DEG) if tab[d][i] == r and d != r] for r in range(n)]
    sup = []
    for d in range(n):
        lst = []
        for i in range(DEG):
            for k in range(DEG):
                if tab[tab[d][i]][k] not in lst:
                    lst.append(tab[tab[d][i]][k])
        sup.append(lst)
    takers2 = [[(d, sup[d].index(r)) for d in range(n) if d != r and r in sup[d]] for r in range(n)]
    direct = [[(d, i) for d, i in takers[r] if topo.may_write(homes[r], homes[d])] for r in range(n)]
    cross = [sorted([(d, i) for d, i in takers[r] if not topo.may_write(homes[r], homes[d])],
                    key=lambda e: -_far(topo, homes[r], homes[e[0]])) for r in range(n)]

    def col(q):
        c = (q % 2) * (Q // 2) + q // 2
        return slice(c * NCOL, (c + 1) * NCOL)

    def tile(i):
        return T.ws[:, i * TILE:(i + 1) * TILE]

    def order(r):
        return sorted(range(DEG), key=lambda i: _far(topo, homes[r], homes[tab[r][i]]))

    def lanes_w(j, q):
        return _count(_fan(topo, workers[j][q], [workers[d][q] for d, _ in takers[j]])[0])

    def lanes_h(j, q):
        return _count(_fan(topo, workers[j][q], [homes[d] for d, _ in takers2[j]])[0])

    def lanes_own(j, q):
        busy = 0
        for m in _fan(topo, workers[j][q], [homes[d] for d, _ in takers2[j]]):
            busy |= m
        return _count(_fan(topo, workers[j][q], [homes[j]], busy)[0])

    def w_lands(j, d):
        if topo.may_write(homes[j], homes[d]):
            return _count(_fan(topo, homes[j], [homes[e] for e, _ in direct[j]])[0])
        for a in range(2):
            part = cross[j][a::2]
            if d in [e for e, _ in part]:
                return sum(_count(_fan(topo, workers[j][q], [homes[e] for e, _ in part])[0]) for q in range(a, Q, 2))

    r = T.rank_of(core)
    if r is not None:
        for a in range(2):
            wave = slice(a * COLS // 2, (a + 1) * COLS // 2)
            g.sync.dma_start(T.xs[:, wave], T.x[:, wave]).then_inc(S["ldx%d" % a], 16)
        g.sync.dma_start(T.ws[:], T.w[:]).then_inc(S.ldw, 16)
        g.vector.memset(T.ones[:], 1.0).then_inc(S.one, 1)
        g.wait_ge(S.one, 1)
        g.affine_select(T.idn[:], T.ones[:], [[-1, TILE]], AluOpType.is_equal, 0.0, 0, 1).then_inc(S.idn, 1)
        sent = 0
        for a in range(2):
            g.wait_ge(S["ldx%d" % a], 16)
            k, _ = _post(g, topo, core, [(workers[r][q], T.xs[:, col(q)], T.o0[:], S.ox) for q in range(a, Q, 2)],
                         S.sent, turn=True)
            sent += k
        g.wait_ge(S.ldw, 16)
        for a in range(2):
            k, _ = _post(g, topo, core, [(workers[r][q], T.ws[:], T.ws[:], S.wl) for q in range(a, Q, 2)], S.sent,
                         turn=True)
            sent += k
        if direct[r]:
            k, _ = _post(g, topo, core, [(homes[d], T.ws[:], T["wn%d" % i][:], S["wa%d" % i]) for d, i in direct[r]],
                         S.sent)
            sent += k
        mine = sup[r]
        total = [0] * len(mine)
        for i in range(DEG):
            for k in range(DEG):
                total[mine.index(tab[tab[r][i]][k])] += 1
        seen = [0] * len(mine)
        copied = [False] * len(mine)
        g.tensor.wait_ge(S.ldw, 16)
        g.tensor.wait_ge(S.idn, 1)
        for i in order(r):
            j = tab[r][i]
            if j == r:
                wb = T.ws
            else:
                g.tensor.wait_ge(S["wa%d" % i], w_lands(j, r))
                wb = T["wn%d" % i]
            for k in range(DEG):
                g.tensor.transpose(T["t%d" % i][:, k * TILE:(k + 1) * TILE], wb[:, k * TILE:(k + 1) * TILE],
                                   T.idn[:]).then_inc(S["tr%d" % i], 1)
            g.vector.wait_ge(S["tr%d" % i], DEG)
            g.vector.tensor_copy(T["wt%d" % i][:], T["t%d" % i][:, 0:DEG * TILE]).then_inc(S["tc%d" % i], 1)
            g.tensor.wait_ge(S["tc%d" % i], 1)
            for k in range(DEG):
                s = mine.index(tab[j][k])
                g.tensor.matmul(T["p%d" % s][:, 0:TILE], T["wt%d" % i][:, k * TILE:(k + 1) * TILE], tile(i),
                                start=(seen[s] == 0), stop=(seen[s] == total[s] - 1)).then_inc(S["bm%d" % s], 1)
                seen[s] += 1
            for s in range(len(mine)):
                if seen[s] == total[s] and not copied[s]:
                    copied[s] = True
                    g.vector.wait_ge(S["bm%d" % s], total[s])
                    g.vector.tensor_copy(T.bt[:, s * TILE:(s + 1) * TILE], T["p%d" % s][:, 0:TILE]).then_inc(S.bc, 1)
        g.tensor.wait_ge(S.bc, len(mine))
        terms = sorted(range(len(mine)), key=lambda s: _far(topo, homes[r], homes[mine[s]]))
        inturn = [q for a in range(2) for q in range(a, Q, 2)]
        for a in range(2):
            for k, s in enumerate(terms):
                m = mine[s]
                for q in range(a, Q, 2):
                    g.tensor.wait_ge(S["g%d_%d" % (q, s)], lanes_own(m, q) if m == r else lanes_h(m, q))
                    g.tensor.matmul(T["p%d" % q][:, 0:NCOL], T.bt[:, s * TILE:(s + 1) * TILE], T["f%d" % s][:, col(q)],
                                    start=(k == 0), stop=(k == len(terms) - 1)).then_inc(S["mf%d" % q], 1)
        for q in inturn:
            g.vector.wait_ge(S["mf%d" % q], len(terms))
            g.vector.tensor_copy(T.ys[:, col(q)], T["p%d" % q][:, 0:NCOL]).then_inc(S["cf%d" % q], 1)
        for q in inturn:
            eng = g.sync if q // 2 == 0 else g.scalar
            eng.wait_ge(S["cf%d" % q], 1)
            eng.dma_start(T.y[:, col(q)], T.ys[:, col(q)]).then_inc(S["st%d" % q], 16)
        for q in inturn:
            eng = g.sync if q // 2 == 0 else g.scalar
            eng.wait_ge(S["st%d" % q], 16)
        g.wait_ge(S.sent, sent)
        return

    for r in range(n):
        if core not in workers[r]:
            continue
        q = workers[r].index(core)
        x_lands = _count(_fan(topo, homes[r], workers[r][q % 2::2])[0])
        wl_lands = x_lands
        sent = 0
        g.wait_ge(S.ox, x_lands)
        k, _ = _post(g, topo, core, [(workers[d][q], T.o0[:], T["l0_%d" % i][:], S["a0_%d" % i])
                                     for d, i in takers[r]], S.sent)
        sent += k
        part = cross[r][q % 2::2]
        if part:
            half = slice((q // 2) * HALF, (q // 2 + 1) * HALF)
            g.wait_ge(S.wl, wl_lands)
            k, _ = _post(g, topo, core, [(homes[d], T.ws[:, half], T["wn%d" % i][:, half], S["wa%d" % i])
                                         for d, i in part], S.sent)
            sent += k
        g.tensor.wait_ge(S.wl, wl_lands)
        terms = order(r)
        for k, i in enumerate(terms):
            j = tab[r][i]
            if j == r:
                g.tensor.wait_ge(S.ox, x_lands)
                rhs = T.o0[:]
            else:
                g.tensor.wait_ge(S["a0_%d" % i], lanes_w(j, q))
                rhs = T["l0_%d" % i][:]
            g.tensor.matmul(T.p0[:, 0:NCOL], tile(i), rhs, start=(k == 0), stop=(k == DEG - 1)).then_inc(S.mm0, 1)
        g.vector.wait_ge(S.mm0, DEG)
        g.vector.tensor_copy(T.o1[:], T.p0[:, 0:NCOL]).then_inc(S.cp1, 1)
        g.wait_ge(S.cp1, 1)
        cols = col(q)
        k, busy = _post(g, topo, core, [(homes[d], T.o1[:], T["f%d" % s][:, cols], S["g%d_%d" % (q, s)])
                                        for d, s in takers2[r]], S.sent)
        sent += k
        if r in sup[r]:
            s = sup[r].index(r)
            k, _ = _post(g, topo, core, [(homes[r], T.o1[:], T["f%d" % s][:, cols], S["g%d_%d" % (q, s)])],
                         S.sent, busy)
            sent += k
        g.wait_ge(S.sent, sent)
        return
